import numpy as np
import ml_dtypes


def mxq(x, axis, fmt="e4m3"):
    dtype, down = {"e4m3": (ml_dtypes.float8_e4m3fn, 7), "e5m2": (ml_dtypes.float8_e5m2, 14)}[fmt]
    v = np.moveaxis(np.asarray(x, np.float32).astype(ml_dtypes.bfloat16).astype(np.float64), axis, -1)
    blocks = v.reshape(v.shape[:-1] + (-1, 32))
    amax = np.abs(blocks).max(-1, keepdims=True)
    byte = np.maximum(np.where(amax > 0, np.frexp(amax)[1] - 1 + 127, 0) - down, 1)
    scale = np.exp2(byte - 127.0)
    codes = (blocks / scale).astype(np.float32).astype(dtype).astype(np.float64)
    return np.moveaxis((codes * scale).reshape(v.shape), -1, axis)


WIDE = False


def mx_kscale(k):
    if not WIDE:
        return np.ones(k)
    levels = np.array([10, -10, 5, -5, 0])
    if k % 512:
        return np.exp2(np.random.permutation(np.resize(levels, k // 32))).repeat(32)
    a = np.empty((k // 512, 16))
    for p in range(k // 512):
        a[p, :8] = np.random.permutation(np.resize(levels, 8))
        for g in range(8):
            far = levels[np.abs(levels - a[p, g]) >= 10]
            a[p, g + 8] = far[np.random.randint(len(far))]
    return np.exp2(a.ravel()).repeat(32)


def f64(x):
    return np.asarray(x).astype(np.float64)


def striped(idx):
    return np.tile(idx.reshape(-1, 16).T, (8, 1)).astype(np.uint16)


def unstriped(offs):
    return offs[:16].T.reshape(-1).astype(np.int64)


def relu(v):
    return np.maximum(v, 0.0)


K, T, E, C, N = 1024, 768, 12, 128, 256


def by_expert(wq, xq):
    return np.concatenate([wq[e].T @ xq[:, e * C:(e + 1) * C] for e in range(E)], axis=1)


def setup_inputs():
    n = np.random.standard_normal
    s = mx_kscale(K)[:, None]
    first = np.random.permutation(np.repeat(np.arange(E), T // E))
    second = (first + 1 + np.random.permutation(np.repeat(np.arange(E - 1), -(-T // (E - 1)))[:T])) % E
    while np.bincount(second, minlength=E).max() != T // E:
        load = np.bincount(second, minlength=E); hi, lo = int(load.argmax()), int(load.argmin())
        t = np.flatnonzero((second == hi) & (first != lo))[0]; second[t] = lo
    slot_token = np.empty(E * C, np.int64); pos = np.empty((2, T), np.int64); fill = np.zeros(E, np.int64)
    place = np.stack([np.random.permutation(C) for _ in range(E)])
    for r, deal in enumerate((first, second)):
        for t in np.random.permutation(T):
            e = deal[t]; j = e * C + place[e, fill[e]]; fill[e] += 1; slot_token[j] = t; pos[r, t] = j
    g = np.random.uniform(0.2, 0.8, T)
    return {
        "xT": (n((K, T)) * s).astype(np.float32),
        "w": (n((E, K, N)) / np.sqrt(K) / s[None]).astype(np.float32),
        "b": (0.3 * n((N, E))).astype(np.float32),
        "gate": np.stack([np.tile(g, (N, 1)), np.tile(1.0 - g, (N, 1))]).astype(np.float32),
        "offs": striped(slot_token),
        "pos1": striped(pos[0]),
        "pos2": striped(pos[1]),
    }


def reference(xT, w, b, gate, offs, pos1, pos2):
    idx = unstriped(offs)
    xq = mxq(f64(xT)[:, idx], 0, "e4m3")
    y = by_expert(mxq(f64(w), 1, "e4m3"), xq)
    y = relu(y + np.repeat(f64(b), C, axis=1))
    return f64(gate[0]) * y[:, unstriped(pos1)] + f64(gate[1]) * y[:, unstriped(pos2)]

@@ -1,0 +1,153 @@
+from contextlib import ExitStack
+
+import concourse.mybir as mybir
+
+F32 = mybir.dt.float32
+BF16 = mybir.dt.bfloat16
+U32 = mybir.dt.uint32
+U16 = mybir.dt.uint16
+U8 = mybir.dt.uint8
+FP8X4 = mybir.dt.float8_e4m3fn_x4
+MULT = mybir.AluOpType.mult
+RELU = mybir.ActivationFunctionType.Relu
+
+P = 128
+PACK = 4
+K, T, E, C, N = 1024, 768, 12, 128, 256
+PASSES = K // (P * PACK)
+BLOCKS = N // P
+SLOTS = E * C
+SLICE = 512
+SLICES = SLOTS // SLICE
+X_CHUNKS = ((0, 512), (512, 256))
+
+FLOPS = 2 * SLOTS * K * N
+
+
+def interleave(copy, grouped, planes):
+    copy(
+        out=grouped.rearrange("p (c i) t -> p c t i", i=4),
+        in_=planes.rearrange("p t (c i) -> p c t i", i=4),
+    )
+
+
+def tile_routed_moe_kernel(tc, xT, w, b, gate, offs, pos1, pos2, out):
+    nc = tc.nc
+    with ExitStack() as ctx:
+        keep = ctx.enter_context(tc.tile_pool(name="keep", bufs=1))
+        raws = ctx.enter_context(tc.tile_pool(name="raws", bufs=9))
+        stage = ctx.enter_context(tc.tile_pool(name="stage", bufs=4))
+        psum = ctx.enter_context(tc.psum_pool(name="psum", bufs=8))
+
+        offs_t = keep.tile([P, SLOTS // 16], U16, name="offs_t")
+        pos1_t = keep.tile([P, T // 16], U16, name="pos1_t")
+        pos2_t = keep.tile([P, T // 16], U16, name="pos2_t")
+        bias = keep.tile([P, BLOCKS, E], F32, name="bias")
+
+        x_view = xT.rearrange("(a p t) n -> a p t n", p=P, t=PACK)
+        w_view = w.rearrange("e (a p t) n -> e a p t n", p=P, t=PACK)
+        x_raw = {}
+        for a in range(PASSES):
+            for c0, width in X_CHUNKS:
+                x_raw[a, c0] = keep.tile([P, PACK, width], F32, name=f"x_raw{a}_{c0}")
+                nc.sync.dma_start(out=x_raw[a, c0][:], in_=x_view[a, :, :, c0 : c0 + width])
+            if a == 0:
+                nc.sync.dma_start(offs_t[:], offs)
+        nc.scalar.dma_start(out=bias[:], in_=b.rearrange("(m p) e -> p m e", p=P))
+
+        w_raw = []
+        for e in range(E):
+            raw = raws.tile([P, PASSES, PACK, N], F32, name="w_raw")
+            for a in range(PASSES):
+                nc.sync.dma_start(out=raw[:, a], in_=w_view[e, a])
+            w_raw.append(raw)
+            if e == 1:
+                nc.sync.dma_start(pos1_t[:], pos1)
+                nc.sync.dma_start(pos2_t[:], pos2)
+        gates = []
+        for m in range(BLOCKS):
+            g = keep.tile([P, 2, T], F32, name=f"gate{m}")
+            nc.sync.dma_start(out=g[:], in_=gate[:, m * P : (m + 1) * P, :].rearrange("r p t -> p r t"))
+            gates.append(g)
+
+        x_words = [keep.tile([P, T], U32, name=f"x_words{a}", align_bytes=64) for a in range(PASSES)]
+        x_bytes = keep.tile([P, T], U8, name="x_bytes", align_bytes=64)
+        nc.gpsimd.memset(x_bytes[:], 0)
+        for a in range(PASSES):
+            for c0, width in X_CHUNKS:
+                grouped = keep.tile([P, width, PACK], BF16, name=f"x_grouped{a}_{c0}", align_bytes=64)
+                copy = nc.vector.tensor_copy if c0 == 0 else nc.scalar.copy
+                interleave(copy, grouped[:], x_raw[a, c0][:])
+                nc.vector.quantize_mx(
+                    out=x_words[a][:, c0 : c0 + width].bitcast(FP8X4),
+                    scales=x_bytes[4 * a : P, c0 : c0 + width],
+                    in_=grouped[:].rearrange("p w t -> p (w t)"),
+                )
+
+        words = [[keep.tile([P, SLICE], U32, name=f"words{a}_{s}", align_bytes=64) for s in range(SLICES)] for a in range(PASSES)]
+        scales = [keep.tile([P, SLICE], U8, name=f"scales{s}", align_bytes=64) for s in range(SLICES)]
+
+        def gather(s):
+            picked = offs_t[:, s * SLICE // 16 : (s + 1) * SLICE // 16]
+            for a in range(PASSES):
+                nc.vector.tensor_copy(words[a][s][:], x_words[a][:].indirect(picked))
+            nc.vector.tensor_copy(scales[s][:], x_bytes[:].indirect(picked))
+
+        y = [keep.tile([P, SLOTS], F32, name=f"y{m}") for m in range(BLOCKS)]
+
+        def prepare(e, c0, width, copies):
+            grouped = stage.tile([P, PASSES, width, PACK], BF16, name=f"grouped{width}", align_bytes=64)
+            if len(copies) == 1:
+                copies[0](
+                    out=grouped[:].rearrange("p a (c i) t -> p a c t i", i=4),
+                    in_=w_raw[e][:].rearrange("p a t (c i) -> p a c t i", i=4),
+                )
+            else:
+                for a in range(PASSES):
+                    interleave(copies[a], grouped[:, a], w_raw[e][:, a, :, c0 : c0 + width])
+            w_words = stage.tile([P, PASSES, width], U32, name=f"w_words{width}", align_bytes=64)
+            w_bytes = stage.tile([P, PASSES, width], U8, name=f"w_bytes{width}", align_bytes=64)
+            nc.vector.quantize_mx(
+                out=w_words[:].rearrange("p a n -> p (a n)").bitcast(FP8X4),
+                scales=w_bytes[:].rearrange("p a n -> p (a n)"),
+                in_=grouped[:].rearrange("p a n t -> p (a n t)"),
+            )
+            return w_words, w_bytes
+
+        def multiply(e, m, w_words, w_bytes, n0):
+            s, j0 = divmod(e * C, SLICE)
+            acc = psum.tile([P, C], F32, name="acc")
+            for a in range(PASSES):
+                nc.tensor.matmul_mx(
+                    out=acc[:],
+                    lhsT=w_words[:, a, n0 : n0 + P].bitcast(FP8X4),
+                    lhsT_scale=w_bytes[:, a, n0 : n0 + P],
+                    rhs=words[a][s][:, j0 : j0 + C].bitcast(FP8X4),
+                    rhs_scale=scales[s][4 * a : P, j0 : j0 + C],
+                    start=(a == 0),
+                    stop=(a == PASSES - 1),
+                )
+            nc.scalar.activation(y[m][:, e * C : (e + 1) * C], acc[:], RELU, bias=bias[:, m, e : e + 1])
+
+        for e in range(E - 1):
+            if e in (0, 2, 4):
+                gather(e // 2)
+            w_words, w_bytes = prepare(e, 0, N, [nc.vector.tensor_copy if e % 3 == 2 else nc.scalar.copy])
+            for m in range(BLOCKS):
+                multiply(e, m, w_words, w_bytes, m * P)
+        for m in range(BLOCKS):
+            w_words, w_bytes = prepare(E - 1, m * P, P, [nc.scalar.copy, nc.vector.tensor_copy])
+            multiply(E - 1, m, w_words, w_bytes, 0)
+
+        for m, pieces in ((0, 1), (1, 2)):
+            width = T // pieces
+            for h in range(pieces):
+                t0 = h * width
+                cols = slice(t0 // 16, (t0 + width) // 16)
+                first = keep.tile([P, width], F32, name=f"first{m}_{h}")
+                second = keep.tile([P, width], F32, name=f"second{m}_{h}")
+                total = keep.tile([P, width], F32, name=f"total{m}_{h}")
+                nc.vector.tensor_tensor(first[:], y[m][:].indirect(pos1_t[:, cols]), gates[m][:, 0, t0 : t0 + width], MULT)
+                nc.vector.tensor_tensor(second[:], y[m][:].indirect(pos2_t[:, cols]), gates[m][:, 1, t0 : t0 + width], MULT)
+                nc.vector.tensor_add(total[:], first[:], second[:])
+                nc.sync.dma_start(out=out[m * P : (m + 1) * P, t0 : t0 + width], in_=total[:])

@@ -9,7 +9,8 @@ U16 = mybir.dt.uint16
 U8 = mybir.dt.uint8
 FP8X4 = mybir.dt.float8_e4m3fn_x4
 MULT = mybir.AluOpType.mult
-RELU = mybir.ActivationFunctionType.Relu
+ADD = mybir.AluOpType.add
+MAX = mybir.AluOpType.max
 
 P = 128
 PACK = 4
@@ -19,6 +20,8 @@ BLOCKS = N // P
 SLOTS = E * C
 SLICE = 512
 SLICES = SLOTS // SLICE
+FIRST = 0
+ON_VECTOR = (4,)
 X_CHUNKS = ((0, 512), (512, 256))
 
 FLOPS = 2 * SLOTS * K * N
@@ -35,7 +38,7 @@ def tile_routed_moe_kernel(tc, xT, w, b, gate, offs, pos1, pos2, out):
     nc = tc.nc
     with ExitStack() as ctx:
         keep = ctx.enter_context(tc.tile_pool(name="keep", bufs=1))
-        raws = ctx.enter_context(tc.tile_pool(name="raws", bufs=9))
+        raws = ctx.enter_context(tc.tile_pool(name="raws", bufs=10))
         stage = ctx.enter_context(tc.tile_pool(name="stage", bufs=4))
         psum = ctx.enter_context(tc.psum_pool(name="psum", bufs=8))
 
@@ -46,22 +49,26 @@ def tile_routed_moe_kernel(tc, xT, w, b, gate, offs, pos1, pos2, out):
 
         x_view = xT.rearrange("(a p t) n -> a p t n", p=P, t=PACK)
         w_view = w.rearrange("e (a p t) n -> e a p t n", p=P, t=PACK)
-        x_raw = {}
-        for a in range(PASSES):
-            for c0, width in X_CHUNKS:
-                x_raw[a, c0] = keep.tile([P, PACK, width], F32, name=f"x_raw{a}_{c0}")
-                nc.sync.dma_start(out=x_raw[a, c0][:], in_=x_view[a, :, :, c0 : c0 + width])
-            if a == 0:
-                nc.sync.dma_start(offs_t[:], offs)
-        nc.scalar.dma_start(out=bias[:], in_=b.rearrange("(m p) e -> p m e", p=P))
-
         w_raw = []
-        for e in range(E):
-            raw = raws.tile([P, PASSES, PACK, N], F32, name="w_raw")
+
+        def load_expert(e):
+            raw = raws.tile([P, PASSES, PACK, N], F32, name="raw")
             for a in range(PASSES):
                 nc.sync.dma_start(out=raw[:, a], in_=w_view[e, a])
             w_raw.append(raw)
-            if e == 1:
+
+        nc.scalar.dma_start(out=bias[:], in_=b.rearrange("(m p) e -> p m e", p=P))
+        x_raw = {}
+        for a in range(PASSES):
+            for c0, width in X_CHUNKS:
+                x_raw[a, c0] = raws.tile([P, PACK, width], F32, name="raw")
+                nc.sync.dma_start(out=x_raw[a, c0][:], in_=x_view[a, :, :, c0 : c0 + width])
+                if a == 0 and c0 == 0:
+                    nc.sync.dma_start(offs_t[:], offs)
+                    load_expert(0)
+        for e in range(1, E):
+            load_expert(e)
+            if e == 3:
                 nc.sync.dma_start(pos1_t[:], pos1)
                 nc.sync.dma_start(pos2_t[:], pos2)
         gates = []
@@ -70,12 +77,36 @@ def tile_routed_moe_kernel(tc, xT, w, b, gate, offs, pos1, pos2, out):
             nc.sync.dma_start(out=g[:], in_=gate[:, m * P : (m + 1) * P, :].rearrange("r p t -> p r t"))
             gates.append(g)
 
+        def prepare(e, c0, width, copies):
+            grouped = stage.tile([P, PASSES, width, PACK], BF16, name="grouped", align_bytes=64, bufs=10)
+            if len(copies) == 1:
+                copies[0](
+                    out=grouped[:].rearrange("p a (c i) t -> p a c t i", i=4),
+                    in_=w_raw[e][:].rearrange("p a t (c i) -> p a c t i", i=4),
+                )
+            else:
+                for a in range(PASSES):
+                    interleave(copies[a], grouped[:, a], w_raw[e][:, a, :, c0 : c0 + width])
+            w_words = stage.tile([P, PASSES, width], U32, name=f"w_words{width}", align_bytes=64, bufs=2 if width == P else 11)
+            w_bytes = stage.tile([P, PASSES, width], U8, name=f"w_bytes{width}", align_bytes=64, bufs=2 if width == P else 11)
+            nc.vector.quantize_mx(
+                out=w_words[:].rearrange("p a n -> p (a n)").bitcast(FP8X4),
+                scales=w_bytes[:].rearrange("p a n -> p (a n)"),
+                in_=grouped[:].rearrange("p a n t -> p (a n t)"),
+            )
+            return w_words, w_bytes
+
+        def prepare_whole(e):
+            return prepare(e, 0, N, [nc.vector.tensor_copy if e in ON_VECTOR else nc.scalar.copy])
+
+        ready = [prepare_whole(e) for e in range(FIRST)]
+
         x_words = [keep.tile([P, T], U32, name=f"x_words{a}", align_bytes=64) for a in range(PASSES)]
         x_bytes = keep.tile([P, T], U8, name="x_bytes", align_bytes=64)
         nc.gpsimd.memset(x_bytes[:], 0)
         for a in range(PASSES):
             for c0, width in X_CHUNKS:
-                grouped = keep.tile([P, width, PACK], BF16, name=f"x_grouped{a}_{c0}", align_bytes=64)
+                grouped = stage.tile([P, width, PACK], BF16, name="grouped", align_bytes=64, bufs=10)
                 copy = nc.vector.tensor_copy if c0 == 0 else nc.scalar.copy
                 interleave(copy, grouped[:], x_raw[a, c0][:])
                 nc.vector.quantize_mx(
@@ -95,25 +126,6 @@ def tile_routed_moe_kernel(tc, xT, w, b, gate, offs, pos1, pos2, out):
 
         y = [keep.tile([P, SLOTS], F32, name=f"y{m}") for m in range(BLOCKS)]
 
-        def prepare(e, c0, width, copies):
-            grouped = stage.tile([P, PASSES, width, PACK], BF16, name=f"grouped{width}", align_bytes=64)
-            if len(copies) == 1:
-                copies[0](
-                    out=grouped[:].rearrange("p a (c i) t -> p a c t i", i=4),
-                    in_=w_raw[e][:].rearrange("p a t (c i) -> p a c t i", i=4),
-                )
-            else:
-                for a in range(PASSES):
-                    interleave(copies[a], grouped[:, a], w_raw[e][:, a, :, c0 : c0 + width])
-            w_words = stage.tile([P, PASSES, width], U32, name=f"w_words{width}", align_bytes=64)
-            w_bytes = stage.tile([P, PASSES, width], U8, name=f"w_bytes{width}", align_bytes=64)
-            nc.vector.quantize_mx(
-                out=w_words[:].rearrange("p a n -> p (a n)").bitcast(FP8X4),
-                scales=w_bytes[:].rearrange("p a n -> p (a n)"),
-                in_=grouped[:].rearrange("p a n t -> p (a n t)"),
-            )
-            return w_words, w_bytes
-
         def multiply(e, m, w_words, w_bytes, n0):
             s, j0 = divmod(e * C, SLICE)
             acc = psum.tile([P, C], F32, name="acc")
@@ -127,14 +139,15 @@ def tile_routed_moe_kernel(tc, xT, w, b, gate, offs, pos1, pos2, out):
                     start=(a == 0),
                     stop=(a == PASSES - 1),
                 )
-            nc.scalar.activation(y[m][:, e * C : (e + 1) * C], acc[:], RELU, bias=bias[:, m, e : e + 1])
+            nc.vector.tensor_scalar(y[m][:, e * C : (e + 1) * C], acc[:], bias[:, m, e : e + 1], 0.0, ADD, MAX)
 
         for e in range(E - 1):
-            if e in (0, 2, 4):
-                gather(e // 2)
-            w_words, w_bytes = prepare(e, 0, N, [nc.vector.tensor_copy if e % 3 == 2 else nc.scalar.copy])
+            if e * C % SLICE == 0:
+                gather(e * C // SLICE)
+            if e >= FIRST:
+                ready.append(prepare_whole(e))
             for m in range(BLOCKS):
-                multiply(e, m, w_words, w_bytes, m * P)
+                multiply(e, m, *ready[e], m * P)
         for m in range(BLOCKS):
             w_words, w_bytes = prepare(E - 1, m * P, P, [nc.scalar.copy, nc.vector.tensor_copy])
             multiply(E - 1, m, w_words, w_bytes, 0)

@@ -9,6 +9,7 @@ U16 = mybir.dt.uint16
 U8 = mybir.dt.uint8
 FP8X4 = mybir.dt.float8_e4m3fn_x4
 MULT = mybir.AluOpType.mult
+RELU = mybir.ActivationFunctionType.Relu
 ADD = mybir.AluOpType.add
 MAX = mybir.AluOpType.max
 
@@ -20,8 +21,8 @@ BLOCKS = N // P
 SLOTS = E * C
 SLICE = 512
 SLICES = SLOTS // SLICE
-FIRST = 0
-ON_VECTOR = (4,)
+ON_VECTOR = (6, 7, 8, 9, 10)
+GROUPS = ((0, 4), (4, 8), (8, 10), (10, 11))
 X_CHUNKS = ((0, 512), (512, 256))
 
 FLOPS = 2 * SLOTS * K * N
@@ -57,7 +58,6 @@ def tile_routed_moe_kernel(tc, xT, w, b, gate, offs, pos1, pos2, out):
                 nc.sync.dma_start(out=raw[:, a], in_=w_view[e, a])
             w_raw.append(raw)
 
-        nc.scalar.dma_start(out=bias[:], in_=b.rearrange("(m p) e -> p m e", p=P))
         x_raw = {}
         for a in range(PASSES):
             for c0, width in X_CHUNKS:
@@ -65,12 +65,13 @@ def tile_routed_moe_kernel(tc, xT, w, b, gate, offs, pos1, pos2, out):
                 nc.sync.dma_start(out=x_raw[a, c0][:], in_=x_view[a, :, :, c0 : c0 + width])
                 if a == 0 and c0 == 0:
                     nc.sync.dma_start(offs_t[:], offs)
-                    load_expert(0)
-        for e in range(1, E):
+        for e in range(E):
             load_expert(e)
             if e == 3:
                 nc.sync.dma_start(pos1_t[:], pos1)
                 nc.sync.dma_start(pos2_t[:], pos2)
+            if e == 7:
+                nc.sync.dma_start(out=bias[:], in_=b.rearrange("(m p) e -> p m e", p=P))
         gates = []
         for m in range(BLOCKS):
             g = keep.tile([P, 2, T], F32, name=f"gate{m}")
@@ -99,8 +100,6 @@ def tile_routed_moe_kernel(tc, xT, w, b, gate, offs, pos1, pos2, out):
         def prepare_whole(e):
             return prepare(e, 0, N, [nc.vector.tensor_copy if e in ON_VECTOR else nc.scalar.copy])
 
-        ready = [prepare_whole(e) for e in range(FIRST)]
-
         x_words = [keep.tile([P, T], U32, name=f"x_words{a}", align_bytes=64) for a in range(PASSES)]
         x_bytes = keep.tile([P, T], U8, name="x_bytes", align_bytes=64)
         nc.gpsimd.memset(x_bytes[:], 0)
@@ -126,12 +125,11 @@ def tile_routed_moe_kernel(tc, xT, w, b, gate, offs, pos1, pos2, out):
 
         y = [keep.tile([P, SLOTS], F32, name=f"y{m}") for m in range(BLOCKS)]
 
-        def multiply(e, m, w_words, w_bytes, n0):
+        def multiply(e, acc, m, w_words, w_bytes, n0):
             s, j0 = divmod(e * C, SLICE)
-            acc = psum.tile([P, C], F32, name="acc")
             for a in range(PASSES):
                 nc.tensor.matmul_mx(
-                    out=acc[:],
+                    out=acc,
                     lhsT=w_words[:, a, n0 : n0 + P].bitcast(FP8X4),
                     lhsT_scale=w_bytes[:, a, n0 : n0 + P],
                     rhs=words[a][s][:, j0 : j0 + C].bitcast(FP8X4),
@@ -139,18 +137,29 @@ def tile_routed_moe_kernel(tc, xT, w, b, gate, offs, pos1, pos2, out):
                     start=(a == 0),
                     stop=(a == PASSES - 1),
                 )
-            nc.vector.tensor_scalar(y[m][:, e * C : (e + 1) * C], acc[:], bias[:, m, e : e + 1], 0.0, ADD, MAX)
 
-        for e in range(E - 1):
-            if e * C % SLICE == 0:
-                gather(e * C // SLICE)
-            if e >= FIRST:
-                ready.append(prepare_whole(e))
-            for m in range(BLOCKS):
-                multiply(e, m, *ready[e], m * P)
+        for first, end in GROUPS:
+            acc = [psum.tile([P, end - first, C], F32, name="acc") for m in range(BLOCKS)]
+            for e in range(first, end):
+                if e * C % SLICE == 0:
+                    gather(e * C // SLICE)
+                codes = prepare_whole(e)
+                for m in range(BLOCKS):
+                    multiply(e, acc[m][:, e - first], m, *codes, m * P)
+            for e in range(first, end):
+                for m in range(BLOCKS):
+                    nc.scalar.activation(
+                        y[m][:, e * C : (e + 1) * C], acc[m][:, e - first], RELU, bias=bias[:, m, e : e + 1]
+                    )
+        last = E - 1
         for m in range(BLOCKS):
-            w_words, w_bytes = prepare(E - 1, m * P, P, [nc.scalar.copy, nc.vector.tensor_copy])
-            multiply(E - 1, m, w_words, w_bytes, 0)
+            acc = psum.tile([P, C], F32, name="acc")
+            codes = prepare(last, m * P, P, [nc.scalar.copy, nc.vector.tensor_copy])
+            multiply(last, acc[:], m, *codes, 0)
+            if m == 0:
+                nc.vector.tensor_scalar(y[m][:, last * C :], acc[:], bias[:, m, last : last + 1], 0.0, ADD, MAX)
+            else:
+                nc.scalar.activation(y[m][:, last * C :], acc[:], RELU, bias=bias[:, m, last : last + 1])
 
         for m, pieces in ((0, 1), (1, 2)):
             width = T // pieces

@@ -21,7 +21,8 @@ BLOCKS = N // P
 SLOTS = E * C
 SLICE = 512
 SLICES = SLOTS // SLICE
-ON_VECTOR = (6, 7, 8, 9, 10)
+ON_VECTOR = (6, 7)
+SHARED = (8, 9, 10)
 GROUPS = ((0, 4), (4, 8), (8, 10), (10, 11))
 X_CHUNKS = ((0, 512), (512, 256))
 
@@ -39,7 +40,7 @@ def tile_routed_moe_kernel(tc, xT, w, b, gate, offs, pos1, pos2, out):
     nc = tc.nc
     with ExitStack() as ctx:
         keep = ctx.enter_context(tc.tile_pool(name="keep", bufs=1))
-        raws = ctx.enter_context(tc.tile_pool(name="raws", bufs=10))
+        raws = ctx.enter_context(tc.tile_pool(name="raws", bufs=7))
         stage = ctx.enter_context(tc.tile_pool(name="stage", bufs=4))
         psum = ctx.enter_context(tc.psum_pool(name="psum", bufs=8))
 
@@ -54,40 +55,52 @@ def tile_routed_moe_kernel(tc, xT, w, b, gate, offs, pos1, pos2, out):
 
         def load_expert(e):
             raw = raws.tile([P, PASSES, PACK, N], F32, name="raw")
-            for a in range(PASSES):
-                nc.sync.dma_start(out=raw[:, a], in_=w_view[e, a])
+            nc.sync.dma_start(out=raw[:], in_=w_view[e].rearrange("a p t n -> p a t n"))
             w_raw.append(raw)
 
-        x_raw = {}
+        x_raw = []
         for a in range(PASSES):
-            for c0, width in X_CHUNKS:
-                x_raw[a, c0] = raws.tile([P, PACK, width], F32, name="raw")
-                nc.sync.dma_start(out=x_raw[a, c0][:], in_=x_view[a, :, :, c0 : c0 + width])
-                if a == 0 and c0 == 0:
-                    nc.sync.dma_start(offs_t[:], offs)
-        for e in range(E):
+            raw = keep.tile([P, PACK, T], F32, name=f"x_raw{a}")
+            nc.sync.dma_start(out=raw[:], in_=x_view[a])
+            x_raw.append(raw)
+        nc.sync.dma_start(offs_t[:], offs)
+        for e in range(E - 1):
             load_expert(e)
             if e == 3:
                 nc.sync.dma_start(pos1_t[:], pos1)
                 nc.sync.dma_start(pos2_t[:], pos2)
-            if e == 7:
+            if e == 6:
                 nc.sync.dma_start(out=bias[:], in_=b.rearrange("(m p) e -> p m e", p=P))
         gates = []
+        w_last = []
         for m in range(BLOCKS):
-            g = keep.tile([P, 2, T], F32, name=f"gate{m}")
-            nc.sync.dma_start(out=g[:], in_=gate[:, m * P : (m + 1) * P, :].rearrange("r p t -> p r t"))
-            gates.append(g)
+            w_last.append(keep.tile([P, PASSES, PACK, P], F32, name=f"w_last{m}"))
+            gates.append(keep.tile([P, 2, T], F32, name=f"gate{m}"))
 
-        def prepare(e, c0, width, copies):
+        def load_last(m):
+            for a in range(PASSES):
+                nc.sync.dma_start(out=w_last[m][:, a], in_=w_view[E - 1, a, :, :, m * P : (m + 1) * P])
+
+        def load_gate(m, r):
+            nc.sync.dma_start(out=gates[m][:, r], in_=gate[r, m * P : (m + 1) * P, :])
+
+        load_last(0)
+        load_gate(0, 0)
+        load_last(1)
+        load_gate(0, 1)
+        load_gate(1, 0)
+        load_gate(1, 1)
+
+        def prepare(raw, width, copies):
             grouped = stage.tile([P, PASSES, width, PACK], BF16, name="grouped", align_bytes=64, bufs=10)
             if len(copies) == 1:
                 copies[0](
                     out=grouped[:].rearrange("p a (c i) t -> p a c t i", i=4),
-                    in_=w_raw[e][:].rearrange("p a t (c i) -> p a c t i", i=4),
+                    in_=raw[:].rearrange("p a t (c i) -> p a c t i", i=4),
                 )
             else:
                 for a in range(PASSES):
-                    interleave(copies[a], grouped[:, a], w_raw[e][:, a, :, c0 : c0 + width])
+                    interleave(copies[a], grouped[:, a], raw[:, a])
             w_words = stage.tile([P, PASSES, width], U32, name=f"w_words{width}", align_bytes=64, bufs=2 if width == P else 11)
             w_bytes = stage.tile([P, PASSES, width], U8, name=f"w_bytes{width}", align_bytes=64, bufs=2 if width == P else 11)
             nc.vector.quantize_mx(
@@ -98,7 +111,9 @@ def tile_routed_moe_kernel(tc, xT, w, b, gate, offs, pos1, pos2, out):
             return w_words, w_bytes
 
         def prepare_whole(e):
-            return prepare(e, 0, N, [nc.vector.tensor_copy if e in ON_VECTOR else nc.scalar.copy])
+            if e in SHARED:
+                return prepare(w_raw[e], N, [nc.scalar.copy, nc.vector.tensor_copy])
+            return prepare(w_raw[e], N, [nc.vector.tensor_copy if e in ON_VECTOR else nc.scalar.copy])
 
         x_words = [keep.tile([P, T], U32, name=f"x_words{a}", align_bytes=64) for a in range(PASSES)]
         x_bytes = keep.tile([P, T], U8, name="x_bytes", align_bytes=64)
@@ -107,7 +122,7 @@ def tile_routed_moe_kernel(tc, xT, w, b, gate, offs, pos1, pos2, out):
             for c0, width in X_CHUNKS:
                 grouped = stage.tile([P, width, PACK], BF16, name="grouped", align_bytes=64, bufs=10)
                 copy = nc.vector.tensor_copy if c0 == 0 else nc.scalar.copy
-                interleave(copy, grouped[:], x_raw[a, c0][:])
+                interleave(copy, grouped[:], x_raw[a][:, :, c0 : c0 + width])
                 nc.vector.quantize_mx(
                     out=x_words[a][:, c0 : c0 + width].bitcast(FP8X4),
                     scales=x_bytes[4 * a : P, c0 : c0 + width],
@@ -154,21 +169,19 @@ def tile_routed_moe_kernel(tc, xT, w, b, gate, offs, pos1, pos2, out):
         last = E - 1
         for m in range(BLOCKS):
             acc = psum.tile([P, C], F32, name="acc")
-            codes = prepare(last, m * P, P, [nc.scalar.copy, nc.vector.tensor_copy])
+            codes = prepare(w_last[m], P, [nc.scalar.copy, nc.scalar.copy if m else nc.vector.tensor_copy])
             multiply(last, acc[:], m, *codes, 0)
             if m == 0:
                 nc.vector.tensor_scalar(y[m][:, last * C :], acc[:], bias[:, m, last : last + 1], 0.0, ADD, MAX)
             else:
                 nc.scalar.activation(y[m][:, last * C :], acc[:], RELU, bias=bias[:, m, last : last + 1])
 
-        for m, pieces in ((0, 1), (1, 2)):
-            width = T // pieces
-            for h in range(pieces):
-                t0 = h * width
+        for m, pieces in ((0, ((0, 768),)), (1, ((0, 512), (512, 256)))):
+            for t0, width in pieces:
                 cols = slice(t0 // 16, (t0 + width) // 16)
-                first = keep.tile([P, width], F32, name=f"first{m}_{h}")
-                second = keep.tile([P, width], F32, name=f"second{m}_{h}")
-                total = keep.tile([P, width], F32, name=f"total{m}_{h}")
+                first = keep.tile([P, width], F32, name=f"first{m}_{t0}")
+                second = keep.tile([P, width], F32, name=f"second{m}_{t0}")
+                total = keep.tile([P, width], F32, name=f"total{m}_{t0}")
                 nc.vector.tensor_tensor(first[:], y[m][:].indirect(pos1_t[:, cols]), gates[m][:, 0, t0 : t0 + width], MULT)
                 nc.vector.tensor_tensor(second[:], y[m][:].indirect(pos2_t[:, cols]), gates[m][:, 1, t0 : t0 + width], MULT)
                 nc.vector.tensor_add(total[:], first[:], second[:])

@@ -1,6 +1,7 @@
 from contextlib import ExitStack
 
 import concourse.mybir as mybir
+from concourse.masks import make_identity
 
 F32 = mybir.dt.float32
 BF16 = mybir.dt.bfloat16
@@ -21,8 +22,7 @@ BLOCKS = N // P
 SLOTS = E * C
 SLICE = 512
 SLICES = SLOTS // SLICE
-ON_VECTOR = (6, 7)
-SHARED = (8, 9, 10)
+ON_VECTOR = (6, 7, 8, 9, 10,)
 GROUPS = ((0, 4), (4, 8), (8, 10), (10, 11))
 X_CHUNKS = ((0, 512), (512, 256))
 
@@ -47,6 +47,8 @@ def tile_routed_moe_kernel(tc, xT, w, b, gate, offs, pos1, pos2, out):
         offs_t = keep.tile([P, SLOTS // 16], U16, name="offs_t")
         pos1_t = keep.tile([P, T // 16], U16, name="pos1_t")
         pos2_t = keep.tile([P, T // 16], U16, name="pos2_t")
+        identity = keep.tile([P, P], F32, name="identity")
+        make_identity(nc, identity[:])
         bias = keep.tile([P, BLOCKS, E], F32, name="bias")
 
         x_view = xT.rearrange("(a p t) n -> a p t n", p=P, t=PACK)
@@ -58,18 +60,21 @@ def tile_routed_moe_kernel(tc, xT, w, b, gate, offs, pos1, pos2, out):
             nc.sync.dma_start(out=raw[:], in_=w_view[e].rearrange("a p t n -> p a t n"))
             w_raw.append(raw)
 
-        x_raw = []
-        for a in range(PASSES):
-            raw = keep.tile([P, PACK, T], F32, name=f"x_raw{a}")
-            nc.sync.dma_start(out=raw[:], in_=x_view[a])
-            x_raw.append(raw)
+        x_first = []
+        for c0, width in X_CHUNKS:
+            raw = keep.tile([P, PACK, width], F32, name=f"x_first{c0}")
+            nc.sync.dma_start(out=raw[:], in_=x_view[0, :, :, c0 : c0 + width])
+            x_first.append(raw)
+        x_second = keep.tile([P, PACK, T], F32, name="x_second")
+        nc.sync.dma_start(out=x_second[:], in_=x_view[1])
         nc.sync.dma_start(offs_t[:], offs)
+        x_planes = [
+            [x_first[0][:], x_first[1][:]],
+            [x_second[:, :, c0 : c0 + width] for c0, width in X_CHUNKS],
+        ]
         for e in range(E - 1):
             load_expert(e)
-            if e == 3:
-                nc.sync.dma_start(pos1_t[:], pos1)
-                nc.sync.dma_start(pos2_t[:], pos2)
-            if e == 6:
+            if e == 7:
                 nc.sync.dma_start(out=bias[:], in_=b.rearrange("(m p) e -> p m e", p=P))
         gates = []
         w_last = []
@@ -85,8 +90,10 @@ def tile_routed_moe_kernel(tc, xT, w, b, gate, offs, pos1, pos2, out):
             nc.sync.dma_start(out=gates[m][:, r], in_=gate[r, m * P : (m + 1) * P, :])
 
         load_last(0)
+        nc.sync.dma_start(pos1_t[:], pos1)
         load_gate(0, 0)
         load_last(1)
+        nc.sync.dma_start(pos2_t[:], pos2)
         load_gate(0, 1)
         load_gate(1, 0)
         load_gate(1, 1)
@@ -111,18 +118,16 @@ def tile_routed_moe_kernel(tc, xT, w, b, gate, offs, pos1, pos2, out):
             return w_words, w_bytes
 
         def prepare_whole(e):
-            if e in SHARED:
-                return prepare(w_raw[e], N, [nc.scalar.copy, nc.vector.tensor_copy])
             return prepare(w_raw[e], N, [nc.vector.tensor_copy if e in ON_VECTOR else nc.scalar.copy])
 
         x_words = [keep.tile([P, T], U32, name=f"x_words{a}", align_bytes=64) for a in range(PASSES)]
         x_bytes = keep.tile([P, T], U8, name="x_bytes", align_bytes=64)
         nc.gpsimd.memset(x_bytes[:], 0)
         for a in range(PASSES):
-            for c0, width in X_CHUNKS:
+            for (c0, width), planes in zip(X_CHUNKS, x_planes[a]):
                 grouped = stage.tile([P, width, PACK], BF16, name="grouped", align_bytes=64, bufs=10)
-                copy = nc.vector.tensor_copy if c0 == 0 else nc.scalar.copy
-                interleave(copy, grouped[:], x_raw[a][:, :, c0 : c0 + width])
+                copy = nc.vector.tensor_copy if (c0 == 0) == (a == 0) else nc.scalar.copy
+                interleave(copy, grouped[:], planes)
                 nc.vector.quantize_mx(
                     out=x_words[a][:, c0 : c0 + width].bitcast(FP8X4),
                     scales=x_bytes[4 * a : P, c0 : c0 + width],
@@ -169,20 +174,29 @@ def tile_routed_moe_kernel(tc, xT, w, b, gate, offs, pos1, pos2, out):
         last = E - 1
         for m in range(BLOCKS):
             acc = psum.tile([P, C], F32, name="acc")
-            codes = prepare(w_last[m], P, [nc.scalar.copy, nc.scalar.copy if m else nc.vector.tensor_copy])
+            codes = prepare(w_last[m], P, [nc.scalar.copy] if m else [nc.scalar.copy, nc.vector.tensor_copy])
             multiply(last, acc[:], m, *codes, 0)
             if m == 0:
                 nc.vector.tensor_scalar(y[m][:, last * C :], acc[:], bias[:, m, last : last + 1], 0.0, ADD, MAX)
             else:
                 nc.scalar.activation(y[m][:, last * C :], acc[:], RELU, bias=bias[:, m, last : last + 1])
 
-        for m, pieces in ((0, ((0, 768),)), (1, ((0, 512), (512, 256)))):
-            for t0, width in pieces:
-                cols = slice(t0 // 16, (t0 + width) // 16)
-                first = keep.tile([P, width], F32, name=f"first{m}_{t0}")
-                second = keep.tile([P, width], F32, name=f"second{m}_{t0}")
-                total = keep.tile([P, width], F32, name=f"total{m}_{t0}")
-                nc.vector.tensor_tensor(first[:], y[m][:].indirect(pos1_t[:, cols]), gates[m][:, 0, t0 : t0 + width], MULT)
-                nc.vector.tensor_tensor(second[:], y[m][:].indirect(pos2_t[:, cols]), gates[m][:, 1, t0 : t0 + width], MULT)
+        def product(name, m, r, t0, width):
+            result = keep.tile([P, width], F32, name=f"{name}{m}_{t0}")
+            cols = slice(t0 // 16, (t0 + width) // 16)
+            picked = y[m][:].indirect((pos1_t, pos2_t)[r][:, cols])
+            nc.vector.tensor_tensor(result[:], picked, gates[m][:, r, t0 : t0 + width], MULT)
+            return result
+
+        for m, t0, width in ((0, 0, 512), (0, 512, 256), (1, 0, 512), (1, 512, 256)):
+            first = product("first", m, 0, t0, width)
+            second = product("second", m, 1, t0, width)
+            total = keep.tile([P, width], F32, name=f"total{m}_{t0}")
+            if (m, t0) == (0, 0):
+                acc = psum.tile([P, width], F32, name="acc")
+                nc.tensor.matmul(acc[:], identity[:], first[:], start=True, stop=False)
+                nc.tensor.matmul(acc[:], identity[:], second[:], start=False, stop=True)
+                nc.scalar.copy(total[:], acc[:])
+            else:
                 nc.vector.tensor_add(total[:], first[:], second[:])
-                nc.sync.dma_start(out=out[m * P : (m + 1) * P, t0 : t0 + width], in_=total[:])
+            nc.sync.dma_start(out=out[m * P : (m + 1) * P, t0 : t0 + width], in_=total[:])

from contextlib import ExitStack

import concourse.mybir as mybir
from concourse.masks import make_identity

F32 = mybir.dt.float32
BF16 = mybir.dt.bfloat16
U32 = mybir.dt.uint32
U16 = mybir.dt.uint16
U8 = mybir.dt.uint8
FP8X4 = mybir.dt.float8_e4m3fn_x4
MULT = mybir.AluOpType.mult
RELU = mybir.ActivationFunctionType.Relu
ADD = mybir.AluOpType.add
MAX = mybir.AluOpType.max

P = 128
PACK = 4
K, T, E, C, N = 1024, 768, 12, 128, 256
PASSES = K // (P * PACK)
BLOCKS = N // P
SLOTS = E * C
SLICE = 512
SLICES = SLOTS // SLICE
ON_VECTOR = (6, 7, 8, 9, 10,)
GROUPS = ((0, 4), (4, 8), (8, 10), (10, 11))
X_CHUNKS = ((0, 512), (512, 256))

FLOPS = 2 * SLOTS * K * N


def interleave(copy, grouped, planes):
    copy(
        out=grouped.rearrange("p (c i) t -> p c t i", i=4),
        in_=planes.rearrange("p t (c i) -> p c t i", i=4),
    )


def tile_routed_moe_kernel(tc, xT, w, b, gate, offs, pos1, pos2, out):
    nc = tc.nc
    with ExitStack() as ctx:
        keep = ctx.enter_context(tc.tile_pool(name="keep", bufs=1))
        raws = ctx.enter_context(tc.tile_pool(name="raws", bufs=7))
        stage = ctx.enter_context(tc.tile_pool(name="stage", bufs=4))
        psum = ctx.enter_context(tc.psum_pool(name="psum", bufs=8))

        offs_t = keep.tile([P, SLOTS // 16], U16, name="offs_t")
        pos1_t = keep.tile([P, T // 16], U16, name="pos1_t")
        pos2_t = keep.tile([P, T // 16], U16, name="pos2_t")
        identity = keep.tile([P, P], F32, name="identity")
        make_identity(nc, identity[:])
        bias = keep.tile([P, BLOCKS, E], F32, name="bias")

        x_view = xT.rearrange("(a p t) n -> a p t n", p=P, t=PACK)
        w_view = w.rearrange("e (a p t) n -> e a p t n", p=P, t=PACK)
        w_raw = []

        def load_expert(e):
            raw = raws.tile([P, PASSES, PACK, N], F32, name="raw")
            nc.sync.dma_start(out=raw[:], in_=w_view[e].rearrange("a p t n -> p a t n"))
            w_raw.append(raw)

        x_first = []
        for c0, width in X_CHUNKS:
            raw = keep.tile([P, PACK, width], F32, name=f"x_first{c0}")
            nc.sync.dma_start(out=raw[:], in_=x_view[0, :, :, c0 : c0 + width])
            x_first.append(raw)
        x_second = keep.tile([P, PACK, T], F32, name="x_second")
        nc.sync.dma_start(out=x_second[:], in_=x_view[1])
        nc.sync.dma_start(offs_t[:], offs)
        x_planes = [
            [x_first[0][:], x_first[1][:]],
            [x_second[:, :, c0 : c0 + width] for c0, width in X_CHUNKS],
        ]
        for e in range(E - 1):
            load_expert(e)
            if e == 7:
                nc.sync.dma_start(out=bias[:], in_=b.rearrange("(m p) e -> p m e", p=P))
        gates = []
        w_last = []
        for m in range(BLOCKS):
            w_last.append(keep.tile([P, PASSES, PACK, P], F32, name=f"w_last{m}"))
            gates.append(keep.tile([P, 2, T], F32, name=f"gate{m}"))

        def load_last(m):
            for a in range(PASSES):
                nc.sync.dma_start(out=w_last[m][:, a], in_=w_view[E - 1, a, :, :, m * P : (m + 1) * P])

        def load_gate(m, r):
            nc.sync.dma_start(out=gates[m][:, r], in_=gate[r, m * P : (m + 1) * P, :])

        load_last(0)
        nc.sync.dma_start(pos1_t[:], pos1)
        load_gate(0, 0)
        load_last(1)
        nc.sync.dma_start(pos2_t[:], pos2)
        load_gate(0, 1)
        load_gate(1, 0)
        load_gate(1, 1)

        def prepare(raw, width, copies):
            grouped = stage.tile([P, PASSES, width, PACK], BF16, name="grouped", align_bytes=64, bufs=10)
            if len(copies) == 1:
                copies[0](
                    out=grouped[:].rearrange("p a (c i) t -> p a c t i", i=4),
                    in_=raw[:].rearrange("p a t (c i) -> p a c t i", i=4),
                )
            else:
                for a in range(PASSES):
                    interleave(copies[a], grouped[:, a], raw[:, a])
            w_words = stage.tile([P, PASSES, width], U32, name=f"w_words{width}", align_bytes=64, bufs=2 if width == P else 11)
            w_bytes = stage.tile([P, PASSES, width], U8, name=f"w_bytes{width}", align_bytes=64, bufs=2 if width == P else 11)
            nc.vector.quantize_mx(
                out=w_words[:].rearrange("p a n -> p (a n)").bitcast(FP8X4),
                scales=w_bytes[:].rearrange("p a n -> p (a n)"),
                in_=grouped[:].rearrange("p a n t -> p (a n t)"),
            )
            return w_words, w_bytes

        def prepare_whole(e):
            return prepare(w_raw[e], N, [nc.vector.tensor_copy if e in ON_VECTOR else nc.scalar.copy])

        x_words = [keep.tile([P, T], U32, name=f"x_words{a}", align_bytes=64) for a in range(PASSES)]
        x_bytes = keep.tile([P, T], U8, name="x_bytes", align_bytes=64)
        nc.gpsimd.memset(x_bytes[:], 0)
        for a in range(PASSES):
            for (c0, width), planes in zip(X_CHUNKS, x_planes[a]):
                grouped = stage.tile([P, width, PACK], BF16, name="grouped", align_bytes=64, bufs=10)
                copy = nc.vector.tensor_copy if (c0 == 0) == (a == 0) else nc.scalar.copy
                interleave(copy, grouped[:], planes)
                nc.vector.quantize_mx(
                    out=x_words[a][:, c0 : c0 + width].bitcast(FP8X4),
                    scales=x_bytes[4 * a : P, c0 : c0 + width],
                    in_=grouped[:].rearrange("p w t -> p (w t)"),
                )

        words = [[keep.tile([P, SLICE], U32, name=f"words{a}_{s}", align_bytes=64) for s in range(SLICES)] for a in range(PASSES)]
        scales = [keep.tile([P, SLICE], U8, name=f"scales{s}", align_bytes=64) for s in range(SLICES)]

        def gather(s):
            picked = offs_t[:, s * SLICE // 16 : (s + 1) * SLICE // 16]
            for a in range(PASSES):
                nc.vector.tensor_copy(words[a][s][:], x_words[a][:].indirect(picked))
            nc.vector.tensor_copy(scales[s][:], x_bytes[:].indirect(picked))

        y = [keep.tile([P, SLOTS], F32, name=f"y{m}") for m in range(BLOCKS)]

        def multiply(e, acc, m, w_words, w_bytes, n0):
            s, j0 = divmod(e * C, SLICE)
            for a in range(PASSES):
                nc.tensor.matmul_mx(
                    out=acc,
                    lhsT=w_words[:, a, n0 : n0 + P].bitcast(FP8X4),
                    lhsT_scale=w_bytes[:, a, n0 : n0 + P],
                    rhs=words[a][s][:, j0 : j0 + C].bitcast(FP8X4),
                    rhs_scale=scales[s][4 * a : P, j0 : j0 + C],
                    start=(a == 0),
                    stop=(a == PASSES - 1),
                )

        for first, end in GROUPS:
            acc = [psum.tile([P, end - first, C], F32, name="acc") for m in range(BLOCKS)]
            for e in range(first, end):
                if e * C % SLICE == 0:
                    gather(e * C // SLICE)
                codes = prepare_whole(e)
                for m in range(BLOCKS):
                    multiply(e, acc[m][:, e - first], m, *codes, m * P)
            for e in range(first, end):
                for m in range(BLOCKS):
                    nc.scalar.activation(
                        y[m][:, e * C : (e + 1) * C], acc[m][:, e - first], RELU, bias=bias[:, m, e : e + 1]
                    )
        last = E - 1
        for m in range(BLOCKS):
            acc = psum.tile([P, C], F32, name="acc")
            codes = prepare(w_last[m], P, [nc.scalar.copy] if m else [nc.scalar.copy, nc.vector.tensor_copy])
            multiply(last, acc[:], m, *codes, 0)
            if m == 0:
                nc.vector.tensor_scalar(y[m][:, last * C :], acc[:], bias[:, m, last : last + 1], 0.0, ADD, MAX)
            else:
                nc.scalar.activation(y[m][:, last * C :], acc[:], RELU, bias=bias[:, m, last : last + 1])

        def product(name, m, r, t0, width):
            result = keep.tile([P, width], F32, name=f"{name}{m}_{t0}")
            cols = slice(t0 // 16, (t0 + width) // 16)
            picked = y[m][:].indirect((pos1_t, pos2_t)[r][:, cols])
            nc.vector.tensor_tensor(result[:], picked, gates[m][:, r, t0 : t0 + width], MULT)
            return result

        for m, t0, width in ((0, 0, 512), (0, 512, 256), (1, 0, 512), (1, 512, 256)):
            first = product("first", m, 0, t0, width)
            second = product("second", m, 1, t0, width)
            total = keep.tile([P, width], F32, name=f"total{m}_{t0}")
            if (m, t0) == (0, 0):
                acc = psum.tile([P, width], F32, name="acc")
                nc.tensor.matmul(acc[:], identity[:], first[:], start=True, stop=False)
                nc.tensor.matmul(acc[:], identity[:], second[:], start=False, stop=True)
                nc.scalar.copy(total[:], acc[:])
            else:
                nc.vector.tensor_add(total[:], first[:], second[:])
            nc.sync.dma_start(out=out[m * P : (m + 1) * P, t0 : t0 + width], in_=total[:])
